import numpy as np
import ml_dtypes


def mxq(x, axis, fmt="e4m3"):
    dtype, down = {"e4m3": (ml_dtypes.float8_e4m3fn, 7), "e5m2": (ml_dtypes.float8_e5m2, 14)}[fmt]
    v = np.moveaxis(np.asarray(x, np.float32).astype(ml_dtypes.bfloat16).astype(np.float64), axis, -1)
    blocks = v.reshape(v.shape[:-1] + (-1, 32))
    amax = np.abs(blocks).max(-1, keepdims=True)
    byte = np.maximum(np.where(amax > 0, np.frexp(amax)[1] - 1 + 127, 0) - down, 1)
    scale = np.exp2(byte - 127.0)
    codes = (blocks / scale).astype(np.float32).astype(dtype).astype(np.float64)
    return np.moveaxis((codes * scale).reshape(v.shape), -1, axis)


WIDE = False


def mx_kscale(k, group=512):
    if not WIDE:
        return np.ones(k)
    levels = np.array([10, -10, 5, -5, 0])
    if group != 512:
        return np.exp2(np.random.permutation(np.resize(levels, k // group))).repeat(group)
    if k % 512:
        return np.exp2(np.random.permutation(np.resize(levels, k // 32))).repeat(32)
    a = np.empty((k // 512, 16))
    for p in range(k // 512):
        a[p, :8] = np.random.permutation(np.resize(levels, 8))
        for g in range(8):
            far = levels[np.abs(levels - a[p, g]) >= 10]
            a[p, g + 8] = far[np.random.randint(len(far))]
    return np.exp2(a.ravel()).repeat(32)


def f64(x):
    return np.asarray(x).astype(np.float64)


def striped(idx):
    return np.tile(np.asarray(idx).reshape(-1, 16).T, (8, 1)).astype(np.uint16)


def unstriped(offs):
    return offs[:16].T.reshape(-1).astype(np.int64)


H, KV, D, NQ, N = 2, 2, 256, 512, 1024
CAP = 2.0


def setup_inputs():
    n = np.random.standard_normal
    s = mx_kscale(D, 0)[:, None]
    u = mx_kscale(N)
    t = np.random.uniform(0.5, 2.0, N) * u
    v = n((KV, N, 128))
    return {
        "qT": (n((H, D, NQ)) * s * (0.70 / np.sqrt(D))).astype(np.float32),
        "kT": (n((KV, D, N)) / s).astype(np.float32),
        "t": t.reshape(N, 1).astype(np.float32),
        "v": (v / t[:, None]).astype(np.float32),
        "mask": (np.arange(N)[:, None] <= np.sort(np.random.randint(N // 4, N, NQ))[None, :]).astype(np.float32),
    }


def reference(qT, kT, t, v, mask):
    a = mxq(f64(kT), 1, "e4m3").transpose(0, 2, 1) @ mxq(f64(qT), 1, "e4m3")
    a = CAP * np.tanh(a / CAP)
    p = 1.0 / (1.0 + np.exp(-a))
    p = p * f64(mask)
    w = p * f64(t)
    y = mxq(w, 1, "e4m3").transpose(0, 2, 1) @ mxq(f64(v), 1, "e4m3")
    y = y / 16.0
    return y

@@ -1,0 +1,254 @@
+from contextlib import ExitStack
+
+import concourse.mybir as mybir
+
+H, D, NQ, N, E = 2, 256, 512, 1024, 128
+FLOPS = 2 * H * N * NQ * (D + E)
+
+F32 = mybir.dt.float32
+BF16 = mybir.dt.bfloat16
+U32 = mybir.dt.uint32
+U8 = mybir.dt.uint8
+FP8X4 = mybir.dt.float8_e4m3fn_x4
+ACT = mybir.ActivationFunctionType
+ALU = mybir.AluOpType
+
+P = 128
+PACK = 4
+ROWS = D // PACK
+PASS = P * PACK
+PASSES = N // PASS
+QC = 128
+CHUNKS = NQ // QC
+UNITS = PASSES * CHUNKS
+BANKS = 2
+RUN = 4
+
+
+def tile_rows_a_sigmoid_mask_cap_kernel(tc, qT, kT, t, v, mask, out):
+    nc = tc.nc
+    with ExitStack() as ctx:
+        sb = ctx.enter_context(tc.tile_pool(name="sb", bufs=1))
+        ps = ctx.enter_context(tc.psum_pool(name="ps", bufs=1))
+        ctx.enter_context(tc.manual_schedule())
+
+        def tile(name, shape, dtype):
+            return sb.tile(shape, dtype, name=name, align_bytes=64)
+
+        q_rows = qT.rearrange("h (p j) q -> (h p) j q", j=PACK)
+        k_rows = kT.rearrange("h (p j) n -> (h p) j n", j=PACK)
+        v_rows = v.rearrange("h (g s j) e -> s (h g) (j e)", g=PASSES, j=PACK)
+        m_rows = mask.rearrange("(g s r) q -> g s r q", g=PASSES, r=PACK)
+        t_rows = t.rearrange("(g s r) o -> s g (r o)", g=PASSES, r=PACK)
+
+        def load(name, src):
+            dst = tile(name, list(src.shape), F32)
+            nc.sync.dma_start(out=dst[:], in_=src)
+            return dst
+
+        warm = tile("warm", [P, 8], F32)
+        nc.gpsimd.memset(warm[:], 0.0)
+        warm_out = tile("warm_out", [P, 8], F32)
+        t_sb = tile("t_sb", [P, PASSES, PACK], F32)
+        nc.scalar.dma_start(out=t_sb[:], in_=t_rows)
+        nc.scalar.activation(out=warm_out[:], in_=warm[:], func=ACT.Sigmoid)
+
+        half = PASS // 2
+        q_first = load("q_first", q_rows[:, :, 0:QC])
+        k0_raw = [load("k0_raw%d" % a, k_rows[:, :, a * half:(a + 1) * half]) for a in range(2)]
+        q_rest = load("q_rest", q_rows[:, :, QC:NQ])
+        m0a = load("m0a", m_rows[0, :, :, 0:NQ // 2])
+        k1_raw = load("k1_raw", k_rows[:, :, PASS:N])
+        m0b = load("m0b", m_rows[0, :, :, NQ // 2:NQ])
+        m1 = load("m1", m_rows[1])
+        v_raw = load("v_raw", v_rows)
+
+        def interleave(copy, dst, src):
+            copy(out=dst.rearrange("p (c i) j -> p c j i", i=RUN), in_=src.rearrange("p j (c i) -> p c j i", i=RUN))
+
+        def quantize(codes, scales, src):
+            nc.vector.quantize_mx(out=codes.bitcast(FP8X4), scales=scales, in_=src)
+
+        q_ops = {}
+
+        def cast_q(name, src):
+            dst = tile(name, [P, src.shape[2], PACK], BF16)
+            interleave(nc.vector.tensor_copy, dst[:], src)
+            return dst
+
+        def quant_q(c0, src):
+            width = src.shape[1]
+            codes = tile("q_codes%d" % c0, [P, width], U32)
+            scales = tile("q_scales%d" % c0, [P, width], U8)
+            quantize(codes[:], scales[:], src[:].rearrange("p q j -> p (q j)"))
+            for i in range(width // QC):
+                q_ops[c0 + i] = (codes, scales, i * QC)
+
+        k_codes = [tile("k_codes%d" % g, [P, PASS], U32) for g in range(PASSES)]
+        k_scales = [tile("k_scales%d" % g, [P, PASS], U8) for g in range(PASSES)]
+
+        def cast_k(copy, name, raw, r0, r1):
+            ns = raw.shape[2] // PACK
+            dst = tile(name, [P, r1 - r0, ns, PACK], BF16)
+            copy(out=dst[:].rearrange("p r s j -> p s j r"),
+                 in_=raw[:].rearrange("p j (s r) -> p s j r", r=PACK)[:, :, :, r0:r1])
+            return dst
+
+        def quant_k_half(a, src, r0):
+            for i in range(src.shape[1]):
+                c0 = (r0 + i) * P + a * (P // 2)
+                quantize(k_codes[0][:, c0:c0 + P // 2], k_scales[0][:, c0:c0 + P // 2],
+                         src[:, i].rearrange("p s j -> p (s j)"))
+
+        mt = {}
+
+        def mask_t(g, raw, c0):
+            width = raw.shape[2]
+            dst = tile("mt%d_%d" % (g, c0), [P, PACK, width], F32)
+            for r in range(PACK):
+                nc.vector.tensor_scalar(out=dst[:, r], in0=raw[:, r], scalar1=t_sb[:, g, r:r + 1], scalar2=None, op0=ALU.mult)
+            for i in range(width // QC):
+                mt[(g, c0 + i)] = (dst, i * QC)
+
+        score = [[ps.tile([P, PACK, QC], F32, name="score%d_%d" % (h, b)) for b in range(BANKS)] for h in range(H)]
+        y_bank = [ps.tile([P, H, 2 * E], F32, name="y%d" % b) for b in range(4)]
+
+        def scores(n):
+            g, c = divmod(n, CHUNKS)
+            codes, scales, q0 = q_ops[c]
+            for h in range(H):
+                rows = slice(h * ROWS, (h + 1) * ROWS)
+                for r in range(PACK):
+                    cols = slice(r * P, (r + 1) * P)
+                    nc.tensor.matmul_mx(out=score[h][n % BANKS][:, r, :],
+                                        lhsT=k_codes[g][rows, cols].bitcast(FP8X4), lhsT_scale=k_scales[g][rows, cols],
+                                        rhs=codes[rows, q0:q0 + QC].bitcast(FP8X4), rhs_scale=scales[rows, q0:q0 + QC],
+                                        start=True, stop=True)
+
+        p_sb = {}
+
+        def weigh(n):
+            capped = []
+            for h in range(H):
+                u = tile("u%d_%d" % (n, h), [P, PACK, QC], F32)
+                nc.scalar.activation(out=u[:], in_=score[h][n % BANKS][:], func=ACT.Tanh, scale=0.5)
+                capped.append(u)
+            for h in range(H):
+                p = tile("p%d_%d" % (n, h), [P, PACK, QC], F32)
+                nc.scalar.activation(out=p[:], in_=capped[h][:], func=ACT.Sigmoid, scale=2.0)
+                p_sb[(n, h)] = p
+
+        w_bf = {}
+
+        def product(n, h):
+            g, c = divmod(n, CHUNKS)
+            if h == 0:
+                w_bf[n] = tile("w_bf%d" % n, [P, H, QC, PACK], BF16)
+            m, q0 = mt[(g, c)]
+            nc.vector.tensor_tensor(out=w_bf[n][:, h].rearrange("p (c i) r -> p c r i", i=RUN),
+                                    in0=p_sb[(n, h)][:].rearrange("p r (c i) -> p c r i", i=RUN),
+                                    in1=m[:, :, q0:q0 + QC].rearrange("p r (c i) -> p c r i", i=RUN), op=ALU.mult)
+
+        w_codes = [tile("w_codes%d" % n, [P, H * QC], U32) for n in range(UNITS)]
+        w_scales = [tile("w_scales%d" % n, [P, H * QC], U8) for n in range(UNITS)]
+
+        def quant_w(n, h0=0, h1=H):
+            quantize(w_codes[n][:, h0 * QC:h1 * QC], w_scales[n][:, h0 * QC:h1 * QC],
+                     w_bf[n][:, h0:h1].rearrange("p h q r -> p (h q r)"))
+
+        v_bf = tile("v_bf", [P, H * PASSES, E, PACK], BF16)
+        v_codes = tile("v_codes", [P, H * PASSES * E], U32)
+        v_scales = tile("v_scales", [P, H * PASSES * E], U8)
+
+        def cast_v(h):
+            x = slice(h * PASSES, (h + 1) * PASSES)
+            nc.vector.tensor_copy(out=v_bf[:, x].rearrange("p x (c i) j -> p x c j i", i=RUN),
+                                  in_=v_raw[:, x].rearrange("p x (j c i) -> p x c j i", j=PACK, i=RUN))
+
+        def values(c, h, g, dst):
+            n = g * CHUNKS + c
+            cols = slice(h * QC, (h + 1) * QC)
+            e0 = (h * PASSES + g) * E
+            nc.tensor.matmul_mx(out=dst, lhsT=w_codes[n][:, cols].bitcast(FP8X4), lhsT_scale=w_scales[n][:, cols],
+                                rhs=v_codes[:, e0:e0 + E].bitcast(FP8X4), rhs_scale=v_scales[:, e0:e0 + E],
+                                start=(g == 0), stop=(g == PASSES - 1))
+
+        def second(c):
+            for h in range(H):
+                for g in range(PASSES):
+                    values(c, h, g, y_bank[c % 2][:, h, 0:E])
+
+        def leave(c):
+            y = tile("y_sb%d" % c, [P, H, E], F32)
+            nc.scalar.activation(out=y[:], in_=y_bank[c % 2][:, :, 0:E], func=ACT.Copy, scale=1.0 / 16.0)
+            nc.sync.dma_start(out=out[:, c * QC:(c + 1) * QC, :].rearrange("h q e -> q h e"), in_=y[:])
+
+        def leave_head(c, h):
+            y = tile("y_last%d" % h, [P, E], F32)
+            nc.scalar.activation(out=y[:], in_=y_bank[2 + h][:, 0, 0:E], func=ACT.Copy, scale=1.0 / 16.0)
+            nc.sync.dma_start(out=out[h, c * QC:(c + 1) * QC, :], in_=y[:])
+
+        q_bf = cast_q("q_bf0", q_first[:])
+        quant_q(0, q_bf)
+        for a in range(2):
+            low = cast_k(nc.vector.tensor_copy, "k0_low%d" % a, k0_raw[a], 0, 2)
+            high = cast_k(nc.scalar.copy, "k0_high%d" % a, k0_raw[a], 2, 4)
+            quant_k_half(a, low, 0)
+            quant_k_half(a, high, 2)
+        scores(0)
+        weigh(0)
+        q_bf = cast_q("q_bf1", q_rest[:, :, 0:QC])
+        quant_q(1, q_bf)
+        scores(1)
+        weigh(1)
+        q_bf = cast_q("q_bf2", q_rest[:, :, QC:3 * QC])
+        mask_t(0, m0a, 0)
+        quant_q(2, q_bf)
+        scores(2)
+        weigh(2)
+        scores(3)
+        weigh(3)
+        product(0, 0)
+        product(0, 1)
+        k1_bf = cast_k(nc.vector.tensor_copy, "k1_bf", k1_raw, 0, PACK)
+        quant_w(0)
+        quantize(k_codes[1][:], k_scales[1][:], k1_bf[:].rearrange("p r s j -> p (r s j)"))
+        for n in range(CHUNKS, UNITS):
+            scores(n)
+            weigh(n)
+        product(1, 0)
+        product(1, 1)
+        mask_t(0, m0b, 2)
+        quant_w(1)
+        product(2, 0)
+        product(2, 1)
+        mask_t(1, m1, 0)
+        quant_w(2)
+        product(3, 0)
+        product(3, 1)
+        cast_v(0)
+        quant_w(3)
+        product(4, 0)
+        product(4, 1)
+        cast_v(1)
+        quant_w(4)
+        quantize(v_codes[:], v_scales[:], v_bf[:].rearrange("p x e j -> p (x e j)"))
+        second(0)
+        product(5, 0)
+        product(5, 1)
+        quant_w(5)
+        second(1)
+        for h in range(H):
+            values(3, h, 0, y_bank[2 + h][:, 0, 0:E])
+        leave(0)
+        product(6, 0)
+        product(6, 1)
+        quant_w(6)
+        second(2)
+        leave(1)
+        leave(2)
+        for h in range(H):
+            product(7, h)
+            quant_w(7, h, h + 1)
+            values(3, h, 1, y_bank[2 + h][:, 0, 0:E])
+            leave_head(3, h)

@@ -56,7 +56,8 @@ def tile_rows_a_sigmoid_mask_cap_kernel(tc, qT, kT, t, v, mask, out):
         half = PASS // 2
         q_first = load("q_first", q_rows[:, :, 0:QC])
         k0_raw = [load("k0_raw%d" % a, k_rows[:, :, a * half:(a + 1) * half]) for a in range(2)]
-        q_rest = load("q_rest", q_rows[:, :, QC:NQ])
+        q_second = load("q_second", q_rows[:, :, QC:2 * QC])
+        q_rest = load("q_rest", q_rows[:, :, 2 * QC:NQ])
         m0a = load("m0a", m_rows[0, :, :, 0:NQ // 2])
         k1_raw = load("k1_raw", k_rows[:, :, PASS:N])
         m0b = load("m0b", m_rows[0, :, :, NQ // 2:NQ])
@@ -102,25 +103,38 @@ def tile_rows_a_sigmoid_mask_cap_kernel(tc, qT, kT, t, v, mask, out):
 
         mt = {}
 
-        def mask_t(g, raw, c0):
+        def mask_tile(g, raw, c0):
             width = raw.shape[2]
             dst = tile("mt%d_%d" % (g, c0), [P, PACK, width], F32)
-            for r in range(PACK):
-                nc.vector.tensor_scalar(out=dst[:, r], in0=raw[:, r], scalar1=t_sb[:, g, r:r + 1], scalar2=None, op0=ALU.mult)
             for i in range(width // QC):
                 mt[(g, c0 + i)] = (dst, i * QC)
+            return dst
+
+        def mask_t_vector(g, raw, dst, places):
+            for r in places:
+                nc.vector.tensor_scalar(out=dst[:, r], in0=raw[:, r], scalar1=t_sb[:, g, r:r + 1], scalar2=None, op0=ALU.mult)
+
+        def mask_t_scalar(g, raw, dst, places):
+            for r in places:
+                nc.scalar.activation(out=dst[:, r], in_=raw[:, r], func=ACT.Copy, scale=t_sb[:, g, r:r + 1])
+
+        def mask_t(g, raw, c0):
+            mask_t_vector(g, raw, mask_tile(g, raw, c0), range(PACK))
 
         score = [[ps.tile([P, PACK, QC], F32, name="score%d_%d" % (h, b)) for b in range(BANKS)] for h in range(H)]
         y_bank = [ps.tile([P, H, 2 * E], F32, name="y%d" % b) for b in range(4)]
 
-        def scores(n):
+        last_bank = [y_bank[0][:, 0, 0:E], y_bank[3][:, 0, 0:E]]
+
+        def scores(n, r0=0, r1=PACK, bank=None):
             g, c = divmod(n, CHUNKS)
             codes, scales, q0 = q_ops[c]
+            bank = (n + 1) % BANKS if bank is None else bank
             for h in range(H):
                 rows = slice(h * ROWS, (h + 1) * ROWS)
-                for r in range(PACK):
+                for r in range(r0, r1):
                     cols = slice(r * P, (r + 1) * P)
-                    nc.tensor.matmul_mx(out=score[h][n % BANKS][:, r, :],
+                    nc.tensor.matmul_mx(out=score[h][bank][:, r, :],
                                         lhsT=k_codes[g][rows, cols].bitcast(FP8X4), lhsT_scale=k_scales[g][rows, cols],
                                         rhs=codes[rows, q0:q0 + QC].bitcast(FP8X4), rhs_scale=scales[rows, q0:q0 + QC],
                                         start=True, stop=True)
@@ -131,8 +145,11 @@ def tile_rows_a_sigmoid_mask_cap_kernel(tc, qT, kT, t, v, mask, out):
             capped = []
             for h in range(H):
                 u = tile("u%d_%d" % (n, h), [P, PACK, QC], F32)
-                nc.scalar.activation(out=u[:], in_=score[h][n % BANKS][:], func=ACT.Tanh, scale=0.5)
                 capped.append(u)
+            parts = [(0, 2, 0), (2, PACK, 1)] if n == 0 else [(0, PACK, (n + 1) % BANKS)]
+            for r0, r1, bank in parts:
+                for h in range(H):
+                    nc.scalar.activation(out=capped[h][:, r0:r1], in_=score[h][bank][:, r0:r1], func=ACT.Tanh, scale=0.5)
             for h in range(H):
                 p = tile("p%d_%d" % (n, h), [P, PACK, QC], F32)
                 nc.scalar.activation(out=p[:], in_=capped[h][:], func=ACT.Sigmoid, scale=2.0)
@@ -176,16 +193,22 @@ def tile_rows_a_sigmoid_mask_cap_kernel(tc, qT, kT, t, v, mask, out):
         def second(c):
             for h in range(H):
                 for g in range(PASSES):
-                    values(c, h, g, y_bank[c % 2][:, h, 0:E])
+                    values(c, h, g, y_bank[c][:, h, 0:E])
 
-        def leave(c):
+        def scale_out(on_vector, dst, src):
+            if on_vector:
+                nc.vector.tensor_scalar(out=dst, in0=src, scalar1=1.0 / 16.0, scalar2=None, op0=ALU.mult)
+            else:
+                nc.scalar.activation(out=dst, in_=src, func=ACT.Copy, scale=1.0 / 16.0)
+
+        def leave(c, on_vector=False):
             y = tile("y_sb%d" % c, [P, H, E], F32)
-            nc.scalar.activation(out=y[:], in_=y_bank[c % 2][:, :, 0:E], func=ACT.Copy, scale=1.0 / 16.0)
+            scale_out(on_vector, y[:], y_bank[c][:, :, 0:E])
             nc.sync.dma_start(out=out[:, c * QC:(c + 1) * QC, :].rearrange("h q e -> q h e"), in_=y[:])
 
-        def leave_head(c, h):
+        def leave_head(c, h, on_vector=False):
             y = tile("y_last%d" % h, [P, E], F32)
-            nc.scalar.activation(out=y[:], in_=y_bank[2 + h][:, 0, 0:E], func=ACT.Copy, scale=1.0 / 16.0)
+            scale_out(on_vector, y[:], last_bank[h])
             nc.sync.dma_start(out=out[h, c * QC:(c + 1) * QC, :], in_=y[:])
 
         q_bf = cast_q("q_bf0", q_first[:])
@@ -195,34 +218,36 @@ def tile_rows_a_sigmoid_mask_cap_kernel(tc, qT, kT, t, v, mask, out):
             high = cast_k(nc.scalar.copy, "k0_high%d" % a, k0_raw[a], 2, 4)
             quant_k_half(a, low, 0)
             quant_k_half(a, high, 2)
-        scores(0)
+        scores(0, 0, 2, 0)
+        scores(0, 2, PACK, 1)
         weigh(0)
-        q_bf = cast_q("q_bf1", q_rest[:, :, 0:QC])
+        q_bf = cast_q("q_bf1", q_second[:])
         quant_q(1, q_bf)
         scores(1)
         weigh(1)
-        q_bf = cast_q("q_bf2", q_rest[:, :, QC:3 * QC])
-        mask_t(0, m0a, 0)
+        q_bf = cast_q("q_bf2", q_rest[:])
         quant_q(2, q_bf)
-        scores(2)
-        weigh(2)
-        scores(3)
-        weigh(3)
+        for n in range(2, CHUNKS):
+            scores(n)
+            weigh(n)
+        mask_t(0, m0a, 0)
         product(0, 0)
         product(0, 1)
-        k1_bf = cast_k(nc.vector.tensor_copy, "k1_bf", k1_raw, 0, PACK)
+        product(1, 0)
         quant_w(0)
+        k1_bf = cast_k(nc.vector.tensor_copy, "k1_bf", k1_raw, 0, PACK)
+        product(1, 1)
         quantize(k_codes[1][:], k_scales[1][:], k1_bf[:].rearrange("p r s j -> p (r s j)"))
+        mt1 = mask_tile(1, m1, 0)
+        mask_t_scalar(1, m1, mt1, range(4, PACK))
         for n in range(CHUNKS, UNITS):
             scores(n)
             weigh(n)
-        product(1, 0)
-        product(1, 1)
         mask_t(0, m0b, 2)
         quant_w(1)
         product(2, 0)
         product(2, 1)
-        mask_t(1, m1, 0)
+        mask_t_vector(1, m1, mt1, range(4))
         quant_w(2)
         product(3, 0)
         product(3, 1)
@@ -232,23 +257,25 @@ def tile_rows_a_sigmoid_mask_cap_kernel(tc, qT, kT, t, v, mask, out):
         product(4, 1)
         cast_v(1)
         quant_w(4)
+        product(5, 0)
         quantize(v_codes[:], v_scales[:], v_bf[:].rearrange("p x e j -> p (x e j)"))
         second(0)
-        product(5, 0)
+        values(3, 1, 0, last_bank[1])
         product(5, 1)
+        product(6, 0)
         quant_w(5)
         second(1)
-        for h in range(H):
-            values(3, h, 0, y_bank[2 + h][:, 0, 0:E])
-        leave(0)
-        product(6, 0)
+        leave(0, False)
+        values(3, 0, 0, last_bank[0])
         product(6, 1)
-        quant_w(6)
-        second(2)
-        leave(1)
-        leave(2)
         for h in range(H):
-            product(7, h)
+            quant_w(6, h, h + 1)
+        second(2)
+        leave(1, False)
+        product(7, 0)
+        leave(2, False)
+        product(7, 1)
+        for h in range(H):
             quant_w(7, h, h + 1)
-            values(3, h, 1, y_bank[2 + h][:, 0, 0:E])
+            values(3, h, 1, last_bank[h])
             leave_head(3, h)

@@ -59,7 +59,7 @@ def tile_rows_a_sigmoid_mask_cap_kernel(tc, qT, kT, t, v, mask, out):
         q_second = load("q_second", q_rows[:, :, QC:2 * QC])
         q_rest = load("q_rest", q_rows[:, :, 2 * QC:NQ])
         m0a = load("m0a", m_rows[0, :, :, 0:NQ // 2])
-        k1_raw = load("k1_raw", k_rows[:, :, PASS:N])
+        k1_raw = [load("k1_raw%d" % a, k_rows[:, :, PASS + a * half:PASS + (a + 1) * half]) for a in range(2)]
         m0b = load("m0b", m_rows[0, :, :, NQ // 2:NQ])
         m1 = load("m1", m_rows[1])
         v_raw = load("v_raw", v_rows)
@@ -121,39 +121,49 @@ def tile_rows_a_sigmoid_mask_cap_kernel(tc, qT, kT, t, v, mask, out):
         def mask_t(g, raw, c0):
             mask_t_vector(g, raw, mask_tile(g, raw, c0), range(PACK))
 
-        score = [[ps.tile([P, PACK, QC], F32, name="score%d_%d" % (h, b)) for b in range(BANKS)] for h in range(H)]
+        score = [ps.tile([P, H, PACK, QC], F32, name="score%d" % b) for b in range(BANKS)]
         y_bank = [ps.tile([P, H, 2 * E], F32, name="y%d" % b) for b in range(4)]
 
         last_bank = [y_bank[0][:, 0, 0:E], y_bank[3][:, 0, 0:E]]
 
-        def scores(n, r0=0, r1=PACK, bank=None):
+        def scores(n):
             g, c = divmod(n, CHUNKS)
             codes, scales, q0 = q_ops[c]
-            bank = (n + 1) % BANKS if bank is None else bank
-            for h in range(H):
+            if n < 1:
+                order = [(h, r) for h in range(H) for r in range(PACK)]
+            else:
+                order = [(h, r) for r in range(PACK) for h in reversed(range(H))]
+            for h, r in order:
                 rows = slice(h * ROWS, (h + 1) * ROWS)
-                for r in range(r0, r1):
-                    cols = slice(r * P, (r + 1) * P)
-                    nc.tensor.matmul_mx(out=score[h][bank][:, r, :],
-                                        lhsT=k_codes[g][rows, cols].bitcast(FP8X4), lhsT_scale=k_scales[g][rows, cols],
-                                        rhs=codes[rows, q0:q0 + QC].bitcast(FP8X4), rhs_scale=scales[rows, q0:q0 + QC],
-                                        start=True, stop=True)
+                cols = slice(r * P, (r + 1) * P)
+                nc.tensor.matmul_mx(out=score[n % BANKS][:, h, r, :],
+                                    lhsT=k_codes[g][rows, cols].bitcast(FP8X4), lhsT_scale=k_scales[g][rows, cols],
+                                    rhs=codes[rows, q0:q0 + QC].bitcast(FP8X4), rhs_scale=scales[rows, q0:q0 + QC],
+                                    start=True, stop=True)
 
-        p_sb = {}
+        capped = [tile("u%d" % n, [P, H, PACK, QC], F32) for n in range(UNITS)]
+        p_sb = [tile("p%d" % n, [P, H, PACK, QC], F32) for n in range(UNITS)]
+        both = slice(0, H)
+        each = [slice(h, h + 1) for h in range(H)]
+
+        def cap(n, heads):
+            nc.scalar.activation(out=capped[n][:, heads], in_=score[n % BANKS][:, heads], func=ACT.Tanh, scale=0.5)
+
+        def gate(n, heads):
+            nc.scalar.activation(out=p_sb[n][:, heads], in_=capped[n][:, heads], func=ACT.Sigmoid, scale=2.0)
 
         def weigh(n):
-            capped = []
-            for h in range(H):
-                u = tile("u%d_%d" % (n, h), [P, PACK, QC], F32)
-                capped.append(u)
-            parts = [(0, 2, 0), (2, PACK, 1)] if n == 0 else [(0, PACK, (n + 1) % BANKS)]
-            for r0, r1, bank in parts:
-                for h in range(H):
-                    nc.scalar.activation(out=capped[h][:, r0:r1], in_=score[h][bank][:, r0:r1], func=ACT.Tanh, scale=0.5)
-            for h in range(H):
-                p = tile("p%d_%d" % (n, h), [P, PACK, QC], F32)
-                nc.scalar.activation(out=p[:], in_=capped[h][:], func=ACT.Sigmoid, scale=2.0)
-                p_sb[(n, h)] = p
+            cap(n, each[0])
+            if 1 < n < UNITS - 1:
+                gate(n - 1, both)
+            if n == UNITS - 1:
+                gate(n - 1, each[1])
+            cap(n, each[1])
+            if n == UNITS - 2:
+                gate(n, each[0])
+            if n in (0, UNITS - 1):
+                for heads in each:
+                    gate(n, heads)
 
         w_bf = {}
 
@@ -163,7 +173,7 @@ def tile_rows_a_sigmoid_mask_cap_kernel(tc, qT, kT, t, v, mask, out):
                 w_bf[n] = tile("w_bf%d" % n, [P, H, QC, PACK], BF16)
             m, q0 = mt[(g, c)]
             nc.vector.tensor_tensor(out=w_bf[n][:, h].rearrange("p (c i) r -> p c r i", i=RUN),
-                                    in0=p_sb[(n, h)][:].rearrange("p r (c i) -> p c r i", i=RUN),
+                                    in0=p_sb[n][:, h].rearrange("p r (c i) -> p c r i", i=RUN),
                                     in1=m[:, :, q0:q0 + QC].rearrange("p r (c i) -> p c r i", i=RUN), op=ALU.mult)
 
         w_codes = [tile("w_codes%d" % n, [P, H * QC], U32) for n in range(UNITS)]
@@ -218,8 +228,7 @@ def tile_rows_a_sigmoid_mask_cap_kernel(tc, qT, kT, t, v, mask, out):
             high = cast_k(nc.scalar.copy, "k0_high%d" % a, k0_raw[a], 2, 4)
             quant_k_half(a, low, 0)
             quant_k_half(a, high, 2)
-        scores(0, 0, 2, 0)
-        scores(0, 2, PACK, 1)
+        scores(0)
         weigh(0)
         q_bf = cast_q("q_bf1", q_second[:])
         quant_q(1, q_bf)
@@ -233,17 +242,19 @@ def tile_rows_a_sigmoid_mask_cap_kernel(tc, qT, kT, t, v, mask, out):
         mask_t(0, m0a, 0)
         product(0, 0)
         product(0, 1)
-        product(1, 0)
+        k1_bf = tile("k1_bf", [P, PACK, P, PACK], BF16)
+        for a in range(2):
+            nc.vector.tensor_copy(out=k1_bf[:, :, a * (P // 2):(a + 1) * (P // 2)].rearrange("p r s j -> p s j r"),
+                                  in_=k1_raw[a][:].rearrange("p j (s r) -> p s j r", r=PACK))
         quant_w(0)
-        k1_bf = cast_k(nc.vector.tensor_copy, "k1_bf", k1_raw, 0, PACK)
-        product(1, 1)
         quantize(k_codes[1][:], k_scales[1][:], k1_bf[:].rearrange("p r s j -> p (r s j)"))
+        product(1, 0)
+        product(1, 1)
+        mask_t(0, m0b, 2)
         mt1 = mask_tile(1, m1, 0)
-        mask_t_scalar(1, m1, mt1, range(4, PACK))
         for n in range(CHUNKS, UNITS):
             scores(n)
             weigh(n)
-        mask_t(0, m0b, 2)
         quant_w(1)
         product(2, 0)
         product(2, 1)
@@ -253,25 +264,25 @@ def tile_rows_a_sigmoid_mask_cap_kernel(tc, qT, kT, t, v, mask, out):
         product(3, 1)
         cast_v(0)
         quant_w(3)
-        product(4, 0)
-        product(4, 1)
         cast_v(1)
-        quant_w(4)
-        product(5, 0)
+        product(4, 0)
         quantize(v_codes[:], v_scales[:], v_bf[:].rearrange("p x e j -> p (x e j)"))
-        second(0)
         values(3, 1, 0, last_bank[1])
+        product(4, 1)
+        product(5, 0)
+        quant_w(4)
+        second(0)
         product(5, 1)
+        leave(0, False)
         product(6, 0)
         quant_w(5)
         second(1)
-        leave(0, False)
-        values(3, 0, 0, last_bank[0])
         product(6, 1)
+        leave(1, False)
         for h in range(H):
             quant_w(6, h, h + 1)
         second(2)
-        leave(1, False)
+        values(3, 0, 0, last_bank[0])
         product(7, 0)
         leave(2, False)
         product(7, 1)

from contextlib import ExitStack

import concourse.mybir as mybir

H, D, NQ, N, E = 2, 256, 512, 1024, 128
FLOPS = 2 * H * N * NQ * (D + E)

F32 = mybir.dt.float32
BF16 = mybir.dt.bfloat16
U32 = mybir.dt.uint32
U8 = mybir.dt.uint8
FP8X4 = mybir.dt.float8_e4m3fn_x4
ACT = mybir.ActivationFunctionType
ALU = mybir.AluOpType

P = 128
PACK = 4
ROWS = D // PACK
PASS = P * PACK
PASSES = N // PASS
QC = 128
CHUNKS = NQ // QC
UNITS = PASSES * CHUNKS
BANKS = 2
RUN = 4


def tile_rows_a_sigmoid_mask_cap_kernel(tc, qT, kT, t, v, mask, out):
    nc = tc.nc
    with ExitStack() as ctx:
        sb = ctx.enter_context(tc.tile_pool(name="sb", bufs=1))
        ps = ctx.enter_context(tc.psum_pool(name="ps", bufs=1))
        ctx.enter_context(tc.manual_schedule())

        def tile(name, shape, dtype):
            return sb.tile(shape, dtype, name=name, align_bytes=64)

        q_rows = qT.rearrange("h (p j) q -> (h p) j q", j=PACK)
        k_rows = kT.rearrange("h (p j) n -> (h p) j n", j=PACK)
        v_rows = v.rearrange("h (g s j) e -> s (h g) (j e)", g=PASSES, j=PACK)
        m_rows = mask.rearrange("(g s r) q -> g s r q", g=PASSES, r=PACK)
        t_rows = t.rearrange("(g s r) o -> s g (r o)", g=PASSES, r=PACK)

        def load(name, src):
            dst = tile(name, list(src.shape), F32)
            nc.sync.dma_start(out=dst[:], in_=src)
            return dst

        warm = tile("warm", [P, 8], F32)
        nc.gpsimd.memset(warm[:], 0.0)
        warm_out = tile("warm_out", [P, 8], F32)
        t_sb = tile("t_sb", [P, PASSES, PACK], F32)
        nc.scalar.dma_start(out=t_sb[:], in_=t_rows)
        nc.scalar.activation(out=warm_out[:], in_=warm[:], func=ACT.Sigmoid)

        half = PASS // 2
        q_first = load("q_first", q_rows[:, :, 0:QC])
        k0_raw = [load("k0_raw%d" % a, k_rows[:, :, a * half:(a + 1) * half]) for a in range(2)]
        q_second = load("q_second", q_rows[:, :, QC:2 * QC])
        q_rest = load("q_rest", q_rows[:, :, 2 * QC:NQ])
        m0a = load("m0a", m_rows[0, :, :, 0:NQ // 2])
        k1_raw = [load("k1_raw%d" % a, k_rows[:, :, PASS + a * half:PASS + (a + 1) * half]) for a in range(2)]
        m0b = load("m0b", m_rows[0, :, :, NQ // 2:NQ])
        m1 = load("m1", m_rows[1])
        v_raw = load("v_raw", v_rows)

        def interleave(copy, dst, src):
            copy(out=dst.rearrange("p (c i) j -> p c j i", i=RUN), in_=src.rearrange("p j (c i) -> p c j i", i=RUN))

        def quantize(codes, scales, src):
            nc.vector.quantize_mx(out=codes.bitcast(FP8X4), scales=scales, in_=src)

        q_ops = {}

        def cast_q(name, src):
            dst = tile(name, [P, src.shape[2], PACK], BF16)
            interleave(nc.vector.tensor_copy, dst[:], src)
            return dst

        def quant_q(c0, src):
            width = src.shape[1]
            codes = tile("q_codes%d" % c0, [P, width], U32)
            scales = tile("q_scales%d" % c0, [P, width], U8)
            quantize(codes[:], scales[:], src[:].rearrange("p q j -> p (q j)"))
            for i in range(width // QC):
                q_ops[c0 + i] = (codes, scales, i * QC)

        k_codes = [tile("k_codes%d" % g, [P, PASS], U32) for g in range(PASSES)]
        k_scales = [tile("k_scales%d" % g, [P, PASS], U8) for g in range(PASSES)]

        def cast_k(copy, name, raw, r0, r1):
            ns = raw.shape[2] // PACK
            dst = tile(name, [P, r1 - r0, ns, PACK], BF16)
            copy(out=dst[:].rearrange("p r s j -> p s j r"),
                 in_=raw[:].rearrange("p j (s r) -> p s j r", r=PACK)[:, :, :, r0:r1])
            return dst

        def quant_k_half(a, src, r0):
            for i in range(src.shape[1]):
                c0 = (r0 + i) * P + a * (P // 2)
                quantize(k_codes[0][:, c0:c0 + P // 2], k_scales[0][:, c0:c0 + P // 2],
                         src[:, i].rearrange("p s j -> p (s j)"))

        mt = {}

        def mask_tile(g, raw, c0):
            width = raw.shape[2]
            dst = tile("mt%d_%d" % (g, c0), [P, PACK, width], F32)
            for i in range(width // QC):
                mt[(g, c0 + i)] = (dst, i * QC)
            return dst

        def mask_t_vector(g, raw, dst, places):
            for r in places:
                nc.vector.tensor_scalar(out=dst[:, r], in0=raw[:, r], scalar1=t_sb[:, g, r:r + 1], scalar2=None, op0=ALU.mult)

        def mask_t_scalar(g, raw, dst, places):
            for r in places:
                nc.scalar.activation(out=dst[:, r], in_=raw[:, r], func=ACT.Copy, scale=t_sb[:, g, r:r + 1])

        def mask_t(g, raw, c0):
            mask_t_vector(g, raw, mask_tile(g, raw, c0), range(PACK))

        score = [ps.tile([P, H, PACK, QC], F32, name="score%d" % b) for b in range(BANKS)]
        y_bank = [ps.tile([P, H, 2 * E], F32, name="y%d" % b) for b in range(4)]

        last_bank = [y_bank[0][:, 0, 0:E], y_bank[3][:, 0, 0:E]]

        def scores(n):
            g, c = divmod(n, CHUNKS)
            codes, scales, q0 = q_ops[c]
            if n < 1:
                order = [(h, r) for h in range(H) for r in range(PACK)]
            else:
                order = [(h, r) for r in range(PACK) for h in reversed(range(H))]
            for h, r in order:
                rows = slice(h * ROWS, (h + 1) * ROWS)
                cols = slice(r * P, (r + 1) * P)
                nc.tensor.matmul_mx(out=score[n % BANKS][:, h, r, :],
                                    lhsT=k_codes[g][rows, cols].bitcast(FP8X4), lhsT_scale=k_scales[g][rows, cols],
                                    rhs=codes[rows, q0:q0 + QC].bitcast(FP8X4), rhs_scale=scales[rows, q0:q0 + QC],
                                    start=True, stop=True)

        capped = [tile("u%d" % n, [P, H, PACK, QC], F32) for n in range(UNITS)]
        p_sb = [tile("p%d" % n, [P, H, PACK, QC], F32) for n in range(UNITS)]
        both = slice(0, H)
        each = [slice(h, h + 1) for h in range(H)]

        def cap(n, heads):
            nc.scalar.activation(out=capped[n][:, heads], in_=score[n % BANKS][:, heads], func=ACT.Tanh, scale=0.5)

        def gate(n, heads):
            nc.scalar.activation(out=p_sb[n][:, heads], in_=capped[n][:, heads], func=ACT.Sigmoid, scale=2.0)

        def weigh(n):
            cap(n, each[0])
            if 1 < n < UNITS - 1:
                gate(n - 1, both)
            if n == UNITS - 1:
                gate(n - 1, each[1])
            cap(n, each[1])
            if n == UNITS - 2:
                gate(n, each[0])
            if n in (0, UNITS - 1):
                for heads in each:
                    gate(n, heads)

        w_bf = {}

        def product(n, h):
            g, c = divmod(n, CHUNKS)
            if h == 0:
                w_bf[n] = tile("w_bf%d" % n, [P, H, QC, PACK], BF16)
            m, q0 = mt[(g, c)]
            nc.vector.tensor_tensor(out=w_bf[n][:, h].rearrange("p (c i) r -> p c r i", i=RUN),
                                    in0=p_sb[n][:, h].rearrange("p r (c i) -> p c r i", i=RUN),
                                    in1=m[:, :, q0:q0 + QC].rearrange("p r (c i) -> p c r i", i=RUN), op=ALU.mult)

        w_codes = [tile("w_codes%d" % n, [P, H * QC], U32) for n in range(UNITS)]
        w_scales = [tile("w_scales%d" % n, [P, H * QC], U8) for n in range(UNITS)]

        def quant_w(n, h0=0, h1=H):
            quantize(w_codes[n][:, h0 * QC:h1 * QC], w_scales[n][:, h0 * QC:h1 * QC],
                     w_bf[n][:, h0:h1].rearrange("p h q r -> p (h q r)"))

        v_bf = tile("v_bf", [P, H * PASSES, E, PACK], BF16)
        v_codes = tile("v_codes", [P, H * PASSES * E], U32)
        v_scales = tile("v_scales", [P, H * PASSES * E], U8)

        def cast_v(h):
            x = slice(h * PASSES, (h + 1) * PASSES)
            nc.vector.tensor_copy(out=v_bf[:, x].rearrange("p x (c i) j -> p x c j i", i=RUN),
                                  in_=v_raw[:, x].rearrange("p x (j c i) -> p x c j i", j=PACK, i=RUN))

        def values(c, h, g, dst):
            n = g * CHUNKS + c
            cols = slice(h * QC, (h + 1) * QC)
            e0 = (h * PASSES + g) * E
            nc.tensor.matmul_mx(out=dst, lhsT=w_codes[n][:, cols].bitcast(FP8X4), lhsT_scale=w_scales[n][:, cols],
                                rhs=v_codes[:, e0:e0 + E].bitcast(FP8X4), rhs_scale=v_scales[:, e0:e0 + E],
                                start=(g == 0), stop=(g == PASSES - 1))

        def second(c):
            for h in range(H):
                for g in range(PASSES):
                    values(c, h, g, y_bank[c][:, h, 0:E])

        def scale_out(on_vector, dst, src):
            if on_vector:
                nc.vector.tensor_scalar(out=dst, in0=src, scalar1=1.0 / 16.0, scalar2=None, op0=ALU.mult)
            else:
                nc.scalar.activation(out=dst, in_=src, func=ACT.Copy, scale=1.0 / 16.0)

        def leave(c, on_vector=False):
            y = tile("y_sb%d" % c, [P, H, E], F32)
            scale_out(on_vector, y[:], y_bank[c][:, :, 0:E])
            nc.sync.dma_start(out=out[:, c * QC:(c + 1) * QC, :].rearrange("h q e -> q h e"), in_=y[:])

        def leave_head(c, h, on_vector=False):
            y = tile("y_last%d" % h, [P, E], F32)
            scale_out(on_vector, y[:], last_bank[h])
            nc.sync.dma_start(out=out[h, c * QC:(c + 1) * QC, :], in_=y[:])

        q_bf = cast_q("q_bf0", q_first[:])
        quant_q(0, q_bf)
        for a in range(2):
            low = cast_k(nc.vector.tensor_copy, "k0_low%d" % a, k0_raw[a], 0, 2)
            high = cast_k(nc.scalar.copy, "k0_high%d" % a, k0_raw[a], 2, 4)
            quant_k_half(a, low, 0)
            quant_k_half(a, high, 2)
        scores(0)
        weigh(0)
        q_bf = cast_q("q_bf1", q_second[:])
        quant_q(1, q_bf)
        scores(1)
        weigh(1)
        q_bf = cast_q("q_bf2", q_rest[:])
        quant_q(2, q_bf)
        for n in range(2, CHUNKS):
            scores(n)
            weigh(n)
        mask_t(0, m0a, 0)
        product(0, 0)
        product(0, 1)
        k1_bf = tile("k1_bf", [P, PACK, P, PACK], BF16)
        for a in range(2):
            nc.vector.tensor_copy(out=k1_bf[:, :, a * (P // 2):(a + 1) * (P // 2)].rearrange("p r s j -> p s j r"),
                                  in_=k1_raw[a][:].rearrange("p j (s r) -> p s j r", r=PACK))
        quant_w(0)
        quantize(k_codes[1][:], k_scales[1][:], k1_bf[:].rearrange("p r s j -> p (r s j)"))
        product(1, 0)
        product(1, 1)
        mask_t(0, m0b, 2)
        mt1 = mask_tile(1, m1, 0)
        for n in range(CHUNKS, UNITS):
            scores(n)
            weigh(n)
        quant_w(1)
        product(2, 0)
        product(2, 1)
        mask_t_vector(1, m1, mt1, range(4))
        quant_w(2)
        product(3, 0)
        product(3, 1)
        cast_v(0)
        quant_w(3)
        cast_v(1)
        product(4, 0)
        quantize(v_codes[:], v_scales[:], v_bf[:].rearrange("p x e j -> p (x e j)"))
        values(3, 1, 0, last_bank[1])
        product(4, 1)
        product(5, 0)
        quant_w(4)
        second(0)
        product(5, 1)
        leave(0, False)
        product(6, 0)
        quant_w(5)
        second(1)
        product(6, 1)
        leave(1, False)
        for h in range(H):
            quant_w(6, h, h + 1)
        second(2)
        values(3, 0, 0, last_bank[0])
        product(7, 0)
        leave(2, False)
        product(7, 1)
        for h in range(H):
            quant_w(7, h, h + 1)
            values(3, h, 1, last_bank[h])
            leave_head(3, h)
